import numpy as np
import ml_dtypes


def mxq(x, axis, fmt="e4m3"):
    dtype, down = {"e4m3": (ml_dtypes.float8_e4m3fn, 7), "e5m2": (ml_dtypes.float8_e5m2, 14)}[fmt]
    v = np.moveaxis(np.asarray(x, np.float32).astype(ml_dtypes.bfloat16).astype(np.float64), axis, -1)
    blocks = v.reshape(v.shape[:-1] + (-1, 32))
    amax = np.abs(blocks).max(-1, keepdims=True)
    byte = np.maximum(np.where(amax > 0, np.frexp(amax)[1] - 1 + 127, 0) - down, 1)
    scale = np.exp2(byte - 127.0)
    codes = (blocks / scale).astype(np.float32).astype(dtype).astype(np.float64)
    return np.moveaxis((codes * scale).reshape(v.shape), -1, axis)


WIDE = False


def mx_kscale(k):
    if not WIDE:
        return np.ones(k)
    levels = np.array([10, -10, 5, -5, 0])
    if k % 512:
        return np.exp2(np.random.permutation(np.resize(levels, k // 32))).repeat(32)
    a = np.empty((k // 512, 16))
    for p in range(k // 512):
        a[p, :8] = np.random.permutation(np.resize(levels, 8))
        for g in range(8):
            far = levels[np.abs(levels - a[p, g]) >= 10]
            a[p, g + 8] = far[np.random.randint(len(far))]
    return np.exp2(a.ravel()).repeat(32)


def f64(x):
    return np.asarray(x).astype(np.float64)


def striped(idx):
    return np.tile(idx.reshape(-1, 16).T, (8, 1)).astype(np.uint16)


def unstriped(offs):
    return offs[:16].T.reshape(-1).astype(np.int64)


E2M1 = np.array([0.0, 0.5, 1.0, 1.5, 2.0, 3.0, 4.0, 6.0, -0.0, -0.5, -1.0, -1.5, -2.0, -3.0, -4.0, -6.0])


def pack_weight(w, fmt):
    k, n = w.shape
    w = f64(np.asarray(w, np.float32).astype(ml_dtypes.bfloat16)).reshape(k // 32, 32, n)
    amax = np.abs(w).max(1)
    if fmt == "e4m3":
        byte = np.frexp(amax)[1] - 1 + 127 - 7
    else:
        mant, ex = np.frexp(amax / 6.0)
        byte = np.where(mant > 0.5, ex, ex - 1) + 127
    byte = np.clip(np.where(amax > 0, byte, 1), 1, 254)
    scaled = (w * np.exp2(127.0 - byte)[:, None, :]).reshape(k, n).astype(np.float32)
    by_word = np.ascontiguousarray(scaled.reshape(k // 512, 128, 4, n).transpose(0, 1, 3, 2))
    if fmt == "e4m3":
        words = by_word.astype(ml_dtypes.float8_e4m3fn).view(np.uint8)
    else:
        c = by_word.astype(ml_dtypes.float4_e2m1fn).view(np.uint8) & 0xF
        words = (c[..., 0::2] | (c[..., 1::2] << 4)).reshape(k // 512, 128, 2 * n)
    return np.ascontiguousarray(words), np.ascontiguousarray(byte.astype(np.uint8).reshape(k // 512, 16, n))


def unpack_weight(words, scales, fmt):
    g, _, n = scales.shape
    words = np.ascontiguousarray(words).reshape(g, 128, n, -1)
    if fmt == "e4m3":
        vals = words.view(ml_dtypes.float8_e4m3fn).astype(np.float64)
    else:
        nib = np.empty((g, 128, n, 4), np.uint8)
        nib[..., 0::2] = words & 0xF
        nib[..., 1::2] = words >> 4
        vals = E2M1[nib]
    vals = vals * np.repeat(np.exp2(scales.astype(np.float64) - 127.0), 8, axis=1)[..., None]
    return vals.transpose(0, 1, 3, 2).reshape(g * 512, n)


def gelu(v):
    return 0.5 * v * (1.0 + np.tanh(np.sqrt(2.0 / np.pi) * (v + 0.044715 * v**3)))


def striped8(idx):
    return np.concatenate([v.reshape(-1, 16).T for v in idx]).astype(np.uint16)


def unstriped8(offs):
    return np.stack([offs[16 * g:16 * g + 16].T.reshape(-1) for g in range(8)]).astype(np.int64)


def heads(h, wgt, idx8):
    r = np.arange(h.shape[0])
    return wgt[r // 4 % 128] * h[r[:, None], idx8[r % 512 // 64]]


def put_heads(h, wgs, idx8, t2):
    r = np.arange(h.shape[0])
    page = np.zeros((h.shape[0], t2))
    page[r[:, None], idx8[r % 512 // 64]] = wgs[r // 4 % 128] * h
    return page


K, H, N, T, S, P, T2 = 1024, 1024, 512, 2048, 1024, 512, 1024

def setup_inputs():
    n = np.random.standard_normal
    s = mx_kscale(K)[:, None]
    u = mx_kscale(H)[:, None]
    d = {}
    d["tab_words"], d["tab_scales"] = pack_weight(n((K, T)) * s, "e4m3")
    d["offs"] = striped(np.random.permutation(T)[:S])
    d["w1"] = (1.5 * n((K, H)) / K ** 0.5 / s * u.T).astype(np.float32)
    d["w2_words"], d["w2_scales"] = pack_weight(n((K, H)) / K ** 0.5 / s * u.T, "e2m1")
    d["unit"] = (np.exp(0.3 * n(H)) * u[:, 0] ** 2).astype(np.float32)
    d["offs2"] = striped8(np.stack([np.random.permutation(S)[:P] for _ in range(8)]))
    d["wgt"] = np.repeat(np.random.uniform(0.5, 2.0, (8, P)), 16, axis=0).astype(np.float32)
    d["shift"] = (n(H) * u[:, 0]).astype(np.float32)
    d["w3"] = (0.45 * n((H, N)) / H ** 0.5 / u).astype(np.float32)
    d["sens"] = np.exp(0.3 * n(N)).astype(np.float32)
    d["climate"] = (0.6 * n((N, P))).astype(np.float32)
    d["offs3"] = striped8(np.stack([np.random.permutation(T2)[:P] for _ in range(8)]))
    d["wgo"] = np.repeat(np.random.uniform(0.5, 2.0, (8, P)), 16, axis=0).astype(np.float32)
    return d

def reference(tab_words, tab_scales, offs, w1, w2_words, w2_scales, unit, offs2, wgt, shift, w3, sens, climate, offs3, wgo):
    v = unpack_weight(tab_words, tab_scales, "e4m3")[:, unstriped(offs)]
    w2 = unpack_weight(w2_words, w2_scales, "e2m1")
    trace = mxq(f64(w1), 0, "e4m3").T @ v
    clean = w2.T @ v
    h = np.sqrt(f64(unit)[:, None] + np.square(trace)) - clean
    x = heads(h, f64(wgt), unstriped8(offs2)) + f64(shift)[:, None]
    need = mxq(f64(w3), 0, "e4m3").T @ mxq(x, 0, "e4m3")
    y = np.tanh(f64(sens)[:, None] * need) + f64(climate)
    return put_heads(y, f64(wgo), unstriped8(offs3), T2)

@@ -1,0 +1,266 @@
+from contextlib import ExitStack
+
+import concourse.mybir as mybir
+
+K, H, N, T, S, M, T2 = 1024, 1024, 512, 2048, 1024, 512, 1024
+FLOPS = 2 * (2 * K * H * S + H * N * M)
+
+F32 = mybir.dt.float32
+BF16 = mybir.dt.bfloat16
+I32 = mybir.dt.int32
+U32 = mybir.dt.uint32
+U16 = mybir.dt.uint16
+U8 = mybir.dt.uint8
+FP8X4 = mybir.dt.float8_e4m3fn_x4
+FP4X4 = mybir.dt.float4_e2m1fn_x4
+ALU = mybir.AluOpType
+ACT = mybir.ActivationFunctionType
+
+P = 128
+PACK = 4
+PASS = P * PACK
+BANK = 512
+SHIFTED = 112
+
+
+def tile_list_pane_treatment_need_kernel(
+    tc, tab_words, tab_scales, offs, w1, w2_words, w2_scales, unit, offs2, wgt, shift, w3, sens, climate, offs3, wgo, out
+):
+    nc = tc.nc
+    with ExitStack() as ctx:
+        keep = ctx.enter_context(tc.tile_pool(name="keep", bufs=1))
+        ring = ctx.enter_context(tc.tile_pool(name="ring", bufs=2))
+        psum = ctx.enter_context(tc.psum_pool(name="psum", bufs=4))
+
+        def held(name, shape, dtype):
+            return keep.tile(shape, dtype, name=name, align_bytes=64)
+
+        tab_sc = keep.tile([P, T], U8, name="tab_sc", tag="tab_sc_then_wgt", align_bytes=64)
+        nc.gpsimd.memset(tab_sc[:].bitcast(I32), 0)
+        w2_sc_raw = held("w2_sc_raw", [P, H], U8)
+        v_sc1 = held("v_sc1", [P, S], U8)
+        w2_sc1 = held("w2_sc1", [P, H], U8)
+        for plane in (w2_sc_raw, v_sc1, w2_sc1):
+            nc.vector.memset(plane[:].bitcast(I32), 0)
+        pages = [held("page%d" % i, [P, T2], F32) for i in range(PACK)]
+        for page in pages:
+            nc.vector.memset(page[:], 0.0)
+        one = held("one", [P, 1], F32)
+        nc.vector.memset(one[:], 1.0)
+        warm = held("warm", [P, 2], F32)
+        nc.scalar.activation(warm[:, 0:1], one[:], ACT.Sqrt)
+
+        def load(name, shape, dtype, src, tag=None, bufs=1):
+            t = keep.tile(shape, dtype, name=name, tag=tag or name, bufs=bufs, align_bytes=64)
+            nc.sync.dma_start(t[:], src)
+            return t
+
+        def load_rows(name, rows):
+            return load(name, [P, PACK, PASS], F32, rows.rearrange("(p j) c -> p j c", j=PACK), "rows", 2)
+
+        def load_w2(b):
+            words = w2_words.bitcast(I32)[:, :, 256 * b : 256 * (b + 1)]
+            return load("w2_raw%d" % b, [P, 2, 256], I32, words.rearrange("a p c -> p a c"), "w2_then_wgo")
+
+        for q in range(4):
+            nc.gpsimd.dma_start(
+                tab_sc[32 * q : 32 * q + 8, :].bitcast(I32), tab_scales.bitcast(I32)[:, 4 * q : 4 * q + 4, :]
+            )
+        for q in range(4):
+            nc.gpsimd.dma_start(
+                w2_sc_raw[32 * q : 32 * q + 8, :].bitcast(I32), w2_scales.bitcast(I32)[:, 4 * q : 4 * q + 4, :]
+            )
+        unit_t = held("unit_t", [P, 2, PACK], F32)
+        shift_t = held("shift_t", [P, 2, PACK], F32)
+        sens_t = held("sens_t", [P, PACK], F32)
+        nc.scalar.dma_start(unit_t[:], unit.rearrange("(b p i) -> p b i", p=P, i=PACK))
+        nc.gpsimd.dma_start(shift_t[:], shift.rearrange("(b p i) -> p b i", p=P, i=PACK))
+        nc.gpsimd.dma_start(sens_t[:], sens.rearrange("(p i) -> p i", i=PACK))
+
+        idx = load("idx", [P, S // 16], U16, offs)
+        def load_tab(a):
+            return load("tab%d" % a, [P, T], I32, tab_words[a].rearrange("p t i -> p (t i)").bitcast(I32))
+
+        def load_w1(a, b):
+            return load_rows("w1_raw%d%d" % (a, b), w1[PASS * a : PASS * (a + 1), PASS * b : PASS * (b + 1)])
+
+        tab, w1_raw, w2_raw = {}, {}, {}
+        tab[0] = load_tab(0)
+        w1_raw[0, 0] = load_w1(0, 0)
+        w2_raw[0] = load_w2(0)
+        w1_raw[1, 0] = load_w1(1, 0)
+        tab[1] = load_tab(1)
+        idx2 = load("idx2", [P, M // 16], U16, offs2)
+        idx3 = load("idx3", [P, M // 16], U16, offs3)
+
+        v_words = [[held("v%d%d" % (a, c), [P, BANK], U32) for c in range(2)] for a in range(2)]
+        v_sc = held("v_sc", [P, S], U8)
+
+        def gather_words(a, c):
+            nc.vector.tensor_copy(v_words[a][c][:], tab[a][:].bitcast(U32).indirect(idx[:, 32 * c : 32 * (c + 1)]))
+
+        gather_words(0, 0)
+        gather_words(0, 1)
+        nc.vector.tensor_copy(v_sc[:], tab_sc[:].indirect(idx[:]))
+        nc.sync.dma_start(v_sc1[0:SHIFTED, :].bitcast(I32), v_sc[4 : 4 + SHIFTED, :].bitcast(I32))
+
+        w2_sc = held("w2_sc", [P, H], U8)
+        nc.vector.tensor_copy(
+            w2_sc[:].rearrange("p (b t m) -> p b m t", b=2, t=PACK),
+            w2_sc_raw[:].rearrange("p (b m t) -> p b m t", b=2, t=PACK),
+        )
+        nc.sync.dma_start(w2_sc1[0:SHIFTED, :].bitcast(I32), w2_sc[4 : 4 + SHIFTED, :].bitcast(I32))
+        wgt_t = load("wgt_t", [P, M], F32, wgt, "tab_sc_then_wgt")
+
+        def cast(copy, grouped, raw, lo, hi):
+            dst = grouped[:].rearrange("p (t m j) -> p m j t", t=PACK, j=PACK)
+            src = raw[:].rearrange("p j (m t) -> p m j t", t=PACK)
+            copy(dst[:, lo:hi], src[:, lo:hi])
+
+        def quantize(grouped, name):
+            width = grouped.shape[1] // PACK
+            codes = held(name + "_codes", [P, width], U32)
+            scales = held(name + "_scales", [P, width], U8)
+            nc.vector.quantize_mx(out=codes[:].bitcast(FP8X4), scales=scales[:], in_=grouped[:])
+            return codes, scales
+
+        def deal_w2(b):
+            dealt = held("w2_dealt%d" % b, [P, 2, 2 * PASS], U8)
+            nc.vector.tensor_copy(
+                dealt[:].bitcast(U16).rearrange("p a (t m) -> p a m t", t=PACK),
+                w2_raw[b][:].bitcast(U16).rearrange("p a (m t) -> p a m t", t=PACK),
+            )
+            return dealt
+
+        w1_bf = {(a, b): held("w1_bf%d%d" % (a, b), [P, PASS * PACK], BF16) for a in range(2) for b in range(2)}
+        w3_bf = [held("w3_bf%d" % b, [P, PASS * PACK], BF16) for b in range(2)]
+        w1_q, w2_q, w3_q, x_q, w3_raw = {}, {}, {}, {}, {}
+        for a in range(2):
+            cast(nc.scalar.copy, w1_bf[a, 0], w1_raw[a, 0], 0, P)
+        w1_q[0, 0] = quantize(w1_bf[0, 0], "w1_00")
+        w2_q[0] = deal_w2(0)
+        gather_words(1, 0)
+        w1_q[1, 0] = quantize(w1_bf[1, 0], "w1_10")
+        gather_words(1, 1)
+        for a in range(2):
+            w1_raw[a, 1] = load_w1(a, 1)
+        w2_raw[1] = load_w2(1)
+
+        def products(b, t, c):
+            rows = slice(P * t, P * (t + 1))
+            cols = slice(BANK * c, BANK * (c + 1))
+            trace = psum.tile([P, BANK], F32, name="trace", bufs=3)
+            for a in range(2):
+                codes, scales = w1_q[a, b]
+                nc.tensor.matmul_mx(
+                    out=trace[:],
+                    lhsT=codes[:, rows].bitcast(FP8X4),
+                    lhsT_scale=scales[:, rows],
+                    rhs=v_words[a][c][:].bitcast(FP8X4),
+                    rhs_scale=v_sc[4 * a : P, cols],
+                    start=(a == 0),
+                    stop=(a == 1),
+                )
+            clean = psum.tile([P, BANK], F32, name="clean", bufs=5)
+            for a in range(2):
+                nc.tensor.matmul_mx(
+                    out=clean[:],
+                    lhsT=w2_q[b][:, a, 2 * P * t : 2 * P * (t + 1)].bitcast(FP4X4),
+                    lhsT_scale=(w2_sc, w2_sc1)[a][:, PASS * b + P * t : PASS * b + P * (t + 1)],
+                    rhs=v_words[a][c][:].bitcast(FP8X4),
+                    rhs_scale=(v_sc, v_sc1)[a][:, cols],
+                    start=(a == 0),
+                    stop=(a == 1),
+                )
+            return trace, clean
+
+        x_rows = [held("x_rows%d" % b, [P, PACK, M], BF16) for b in range(2)]
+
+        def pick(b, t, h, picked):
+            nc.vector.tensor_tensor(picked[:], h[:].indirect(idx2[:]), wgt_t[:], ALU.mult)
+
+        def add_shift(b, t, picked):
+            nc.scalar.activation(x_rows[b][:, t, :], picked[:], ACT.Identity, bias=shift_t[:, b, t : t + 1])
+
+        def weave(b):
+            grouped = held("x_bf%d" % b, [P, M * PACK], BF16)
+            nc.vector.tensor_copy(
+                grouped[:].rearrange("p (c i t) -> p c t i", i=4, t=PACK),
+                x_rows[b][:].rearrange("p t (c i) -> p c t i", i=4),
+            )
+            return grouped
+
+        def side_work(step):
+            half = P // 2
+            if step < 2:
+                cast(nc.scalar.copy, w1_bf[step, 1], w1_raw[step, 1], 0, P)
+                w1_q[step, 1] = quantize(w1_bf[step, 1], "w1_%d1" % step)
+                w3_raw[step] = load_rows("w3_raw%d" % step, w3[PASS * step : PASS * (step + 1), :])
+            if step == 2:
+                w2_q[1] = deal_w2(1)
+            if step in (3, 4, 5, 6):
+                b, part = divmod(step - 3, 2)
+                cast(nc.scalar.copy, w3_bf[b], w3_raw[b], half * part, half * (part + 1))
+                if part == 1:
+                    w3_q[b] = quantize(w3_bf[b], "w3_%d" % b)
+            if step == 6:
+                x_q[0] = quantize(weave(0), "x0")
+
+        tiles = [(b, t) for b in range(2) for t in range(PACK)]
+        to_pick, to_shift = None, None
+        for step, (b, t) in enumerate(tiles):
+            h = ring.tile([P, S], F32, name="h", bufs=3)
+            sums = [products(b, t, c) for c in range(2)]
+            squares = []
+            for c in range(2):
+                sq = ring.tile([P, BANK], F32, name="sq", bufs=6)
+                nc.scalar.activation(sq[:], sums[c][0][:], ACT.Square)
+                squares.append(sq)
+            for c in range(2):
+                root = ring.tile([P, BANK], F32, name="root", bufs=5)
+                nc.scalar.activation(root[:], squares[c][:], ACT.Sqrt, bias=unit_t[:, b, t : t + 1])
+                nc.vector.tensor_tensor(h[:, BANK * c : BANK * (c + 1)], root[:], sums[c][1][:], ALU.subtract)
+                if c == 0 and to_pick is not None:
+                    pick(*to_pick, squares[0])
+            if to_shift is not None:
+                add_shift(*to_shift)
+            if to_pick is not None:
+                to_shift = (to_pick[0], to_pick[1], squares[0])
+            to_pick = (b, t, h)
+            side_work(step)
+        nc.scalar.activation(warm[:, 1:2], root[:, 0:1], ACT.Tanh)
+        add_shift(*to_shift)
+        pick(*to_pick, squares[1])
+        add_shift(to_pick[0], to_pick[1], squares[1])
+        x_q[1] = quantize(weave(1), "x1")
+        wgo_t = load("wgo_t", [P, M], F32, wgo, "w2_then_wgo")
+        clim = load_rows("clim", climate)
+
+        out_rows = out.rearrange("(p i) c -> p i c", i=PACK)
+
+        def place(i, y):
+            nc.vector.tensor_tensor(pages[i][:].indirect(idx3[:]), y[:], wgo_t[:], ALU.mult)
+            nc.sync.dma_start(out_rows[:, i, :], pages[i][:])
+
+        to_place = None
+        for i in range(PACK):
+            rows = slice(P * i, P * (i + 1))
+            need = psum.tile([P, M], F32, name="clean", bufs=5)
+            for b in range(2):
+                nc.tensor.matmul_mx(
+                    out=need[:],
+                    lhsT=w3_q[b][0][:, rows].bitcast(FP8X4),
+                    lhsT_scale=w3_q[b][1][:, rows],
+                    rhs=x_q[b][0][:].bitcast(FP8X4),
+                    rhs_scale=x_q[b][1][:],
+                    start=(b == 0),
+                    stop=(b == 1),
+                )
+            score = ring.tile([P, M], F32, name="score", bufs=4)
+            nc.scalar.activation(score[:], need[:], ACT.Tanh, scale=sens_t[:, i : i + 1])
+            y = ring.tile([P, M], F32, name="y", bufs=4)
+            nc.vector.tensor_tensor(y[:], score[:], clim[:, i, :], ALU.add)
+            if to_place is not None:
+                place(*to_place)
+            to_place = (i, y)
+        place(*to_place)

@@ -32,23 +32,20 @@ def tile_list_pane_treatment_need_kernel(
         ring = ctx.enter_context(tc.tile_pool(name="ring", bufs=2))
         psum = ctx.enter_context(tc.psum_pool(name="psum", bufs=4))
 
-        def held(name, shape, dtype):
-            return keep.tile(shape, dtype, name=name, align_bytes=64)
+        def held(name, shape, dtype, tag=None):
+            return keep.tile(shape, dtype, name=name, tag=tag or name, align_bytes=64)
 
-        tab_sc = keep.tile([P, T], U8, name="tab_sc", tag="tab_sc_then_wgt", align_bytes=64)
-        nc.gpsimd.memset(tab_sc[:].bitcast(I32), 0)
+        tab_sc = keep.tile([P, T], U8, name="tab_sc", tag="tab_sc", align_bytes=64)
         w2_sc_raw = held("w2_sc_raw", [P, H], U8)
+        nc.gpsimd.memset(w2_sc_raw[:].bitcast(I32), 0)
+        nc.gpsimd.memset(tab_sc[:].bitcast(I32), 0)
         v_sc1 = held("v_sc1", [P, S], U8)
         w2_sc1 = held("w2_sc1", [P, H], U8)
-        for plane in (w2_sc_raw, v_sc1, w2_sc1):
+        for plane in (v_sc1, w2_sc1):
             nc.vector.memset(plane[:].bitcast(I32), 0)
-        pages = [held("page%d" % i, [P, T2], F32) for i in range(PACK)]
-        for page in pages:
-            nc.vector.memset(page[:], 0.0)
         one = held("one", [P, 1], F32)
         nc.vector.memset(one[:], 1.0)
         warm = held("warm", [P, 2], F32)
-        nc.scalar.activation(warm[:, 0:1], one[:], ACT.Sqrt)
 
         def load(name, shape, dtype, src, tag=None, bufs=1):
             t = keep.tile(shape, dtype, name=name, tag=tag or name, bufs=bufs, align_bytes=64)
@@ -67,15 +64,10 @@ def tile_list_pane_treatment_need_kernel(
                 tab_sc[32 * q : 32 * q + 8, :].bitcast(I32), tab_scales.bitcast(I32)[:, 4 * q : 4 * q + 4, :]
             )
         for q in range(4):
-            nc.gpsimd.dma_start(
+            nc.scalar.dma_start(
                 w2_sc_raw[32 * q : 32 * q + 8, :].bitcast(I32), w2_scales.bitcast(I32)[:, 4 * q : 4 * q + 4, :]
             )
-        unit_t = held("unit_t", [P, 2, PACK], F32)
-        shift_t = held("shift_t", [P, 2, PACK], F32)
-        sens_t = held("sens_t", [P, PACK], F32)
-        nc.scalar.dma_start(unit_t[:], unit.rearrange("(b p i) -> p b i", p=P, i=PACK))
-        nc.gpsimd.dma_start(shift_t[:], shift.rearrange("(b p i) -> p b i", p=P, i=PACK))
-        nc.gpsimd.dma_start(sens_t[:], sens.rearrange("(p i) -> p i", i=PACK))
+        nc.scalar.activation(warm[:, 0:1], one[:], ACT.Sqrt)
 
         idx = load("idx", [P, S // 16], U16, offs)
         def load_tab(a):
@@ -90,36 +82,39 @@ def tile_list_pane_treatment_need_kernel(
         w2_raw[0] = load_w2(0)
         w1_raw[1, 0] = load_w1(1, 0)
         tab[1] = load_tab(1)
+        unit_t = load("unit_t", [P, 2, PACK], F32, unit.rearrange("(b p i) -> p b i", p=P, i=PACK))
         idx2 = load("idx2", [P, M // 16], U16, offs2)
+        shift_t = load("shift_t", [P, 2, PACK], F32, shift.rearrange("(b p i) -> p b i", p=P, i=PACK))
         idx3 = load("idx3", [P, M // 16], U16, offs3)
+        sens_t = load("sens_t", [P, PACK], F32, sens.rearrange("(p i) -> p i", i=PACK))
 
-        v_words = [[held("v%d%d" % (a, c), [P, BANK], U32) for c in range(2)] for a in range(2)]
+        v_words = {}
         v_sc = held("v_sc", [P, S], U8)
 
-        def gather_words(a, c):
-            nc.vector.tensor_copy(v_words[a][c][:], tab[a][:].bitcast(U32).indirect(idx[:, 32 * c : 32 * (c + 1)]))
+        def gather_words(a, c, tag=None):
+            v_words[a, c] = held("v%d%d" % (a, c), [P, BANK], U32, tag)
+            nc.vector.tensor_copy(v_words[a, c][:], tab[a][:].bitcast(U32).indirect(idx[:, 32 * c : 32 * (c + 1)]))
 
         gather_words(0, 0)
         gather_words(0, 1)
         nc.vector.tensor_copy(v_sc[:], tab_sc[:].indirect(idx[:]))
         nc.sync.dma_start(v_sc1[0:SHIFTED, :].bitcast(I32), v_sc[4 : 4 + SHIFTED, :].bitcast(I32))
 
-        w2_sc = held("w2_sc", [P, H], U8)
+        w2_sc = held("w2_sc", [P, H], U8, "tab0")
         nc.vector.tensor_copy(
             w2_sc[:].rearrange("p (b t m) -> p b m t", b=2, t=PACK),
             w2_sc_raw[:].rearrange("p (b m t) -> p b m t", b=2, t=PACK),
         )
         nc.sync.dma_start(w2_sc1[0:SHIFTED, :].bitcast(I32), w2_sc[4 : 4 + SHIFTED, :].bitcast(I32))
-        wgt_t = load("wgt_t", [P, M], F32, wgt, "tab_sc_then_wgt")
 
         def cast(copy, grouped, raw, lo, hi):
             dst = grouped[:].rearrange("p (t m j) -> p m j t", t=PACK, j=PACK)
             src = raw[:].rearrange("p j (m t) -> p m j t", t=PACK)
             copy(dst[:, lo:hi], src[:, lo:hi])
 
-        def quantize(grouped, name):
+        def quantize(grouped, name, tag=None):
             width = grouped.shape[1] // PACK
-            codes = held(name + "_codes", [P, width], U32)
+            codes = held(name + "_codes", [P, width], U32, tag)
             scales = held(name + "_scales", [P, width], U8)
             nc.vector.quantize_mx(out=codes[:].bitcast(FP8X4), scales=scales[:], in_=grouped[:])
             return codes, scales
@@ -134,13 +129,14 @@ def tile_list_pane_treatment_need_kernel(
 
         w1_bf = {(a, b): held("w1_bf%d%d" % (a, b), [P, PASS * PACK], BF16) for a in range(2) for b in range(2)}
         w3_bf = [held("w3_bf%d" % b, [P, PASS * PACK], BF16) for b in range(2)]
-        w1_q, w2_q, w3_q, x_q, w3_raw = {}, {}, {}, {}, {}
+        w1_q, w2_q, w3_q, w3_raw = {}, {}, {}, {}
         for a in range(2):
             cast(nc.scalar.copy, w1_bf[a, 0], w1_raw[a, 0], 0, P)
-        w1_q[0, 0] = quantize(w1_bf[0, 0], "w1_00")
+        w1_q[0, 0] = quantize(w1_bf[0, 0], "w1_00", "tab_sc")
+        wgt_t = load("wgt_t", [P, M], F32, wgt, "w1_bf00")
         w2_q[0] = deal_w2(0)
-        gather_words(1, 0)
         w1_q[1, 0] = quantize(w1_bf[1, 0], "w1_10")
+        gather_words(1, 0, "w1_bf10")
         gather_words(1, 1)
         for a in range(2):
             w1_raw[a, 1] = load_w1(a, 1)
@@ -156,7 +152,7 @@ def tile_list_pane_treatment_need_kernel(
                     out=trace[:],
                     lhsT=codes[:, rows].bitcast(FP8X4),
                     lhsT_scale=scales[:, rows],
-                    rhs=v_words[a][c][:].bitcast(FP8X4),
+                    rhs=v_words[a, c][:].bitcast(FP8X4),
                     rhs_scale=v_sc[4 * a : P, cols],
                     start=(a == 0),
                     stop=(a == 1),
@@ -167,7 +163,7 @@ def tile_list_pane_treatment_need_kernel(
                     out=clean[:],
                     lhsT=w2_q[b][:, a, 2 * P * t : 2 * P * (t + 1)].bitcast(FP4X4),
                     lhsT_scale=(w2_sc, w2_sc1)[a][:, PASS * b + P * t : PASS * b + P * (t + 1)],
-                    rhs=v_words[a][c][:].bitcast(FP8X4),
+                    rhs=v_words[a, c][:].bitcast(FP8X4),
                     rhs_scale=(v_sc, v_sc1)[a][:, cols],
                     start=(a == 0),
                     stop=(a == 1),
@@ -176,19 +172,36 @@ def tile_list_pane_treatment_need_kernel(
 
         x_rows = [held("x_rows%d" % b, [P, PACK, M], BF16) for b in range(2)]
 
-        def pick(b, t, h, picked):
-            nc.vector.tensor_tensor(picked[:], h[:].indirect(idx2[:]), wgt_t[:], ALU.mult)
-
-        def add_shift(b, t, picked):
-            nc.scalar.activation(x_rows[b][:, t, :], picked[:], ACT.Identity, bias=shift_t[:, b, t : t + 1])
-
-        def weave(b):
-            grouped = held("x_bf%d" % b, [P, M * PACK], BF16)
-            nc.vector.tensor_copy(
-                grouped[:].rearrange("p (c i t) -> p c t i", i=4, t=PACK),
-                x_rows[b][:].rearrange("p t (c i) -> p c t i", i=4),
+        def pick(b, t, h, picked, lo, hi):
+            nc.vector.tensor_tensor(
+                picked[:, lo:hi], h[:].indirect(idx2[:, lo // 16 : hi // 16]), wgt_t[:, lo:hi], ALU.mult
             )
-            return grouped
+            add_shift(b, t, picked, lo, hi)
+
+        def add_shift(b, t, picked, lo, hi):
+            nc.gpsimd.tensor_scalar(
+                x_rows[b][:, t, lo:hi], picked[:, lo:hi], 1.0, shift_t[:, b, t : t + 1], ALU.mult, ALU.add
+            )
+
+        x_bf = [held("x_bf%d" % b, [P, M * PACK], BF16) for b in range(2)]
+        x_q = [(held("x_codes%d" % b, [P, M], U32), held("x_scales%d" % b, [P, M], U8)) for b in range(2)]
+
+        def weave(copy, b, lo, hi):
+            copy(
+                x_bf[b][:, PACK * lo : PACK * hi].rearrange("p (c i t) -> p c t i", i=4, t=PACK),
+                x_rows[b][:, :, lo:hi].rearrange("p t (c i) -> p c t i", i=4),
+            )
+
+        def quantize_x(b, lo, hi):
+            nc.vector.quantize_mx(
+                out=x_q[b][0][:, lo:hi].bitcast(FP8X4), scales=x_q[b][1][:, lo:hi], in_=x_bf[b][:, PACK * lo : PACK * hi]
+            )
+
+        pages = {}
+
+        def clear_page(i, tag):
+            pages[i] = held("page%d" % i, [P, T2], F32, tag)
+            nc.gpsimd.memset(pages[i][:], 0.0)
 
         def side_work(step):
             half = P // 2
@@ -203,64 +216,72 @@ def tile_list_pane_treatment_need_kernel(
                 cast(nc.scalar.copy, w3_bf[b], w3_raw[b], half * part, half * (part + 1))
                 if part == 1:
                     w3_q[b] = quantize(w3_bf[b], "w3_%d" % b)
+            if step == 5:
+                weave(nc.scalar.copy, 0, 0, M // 2)
+                weave(nc.vector.tensor_copy, 0, M // 2, M)
             if step == 6:
-                x_q[0] = quantize(weave(0), "x0")
+                quantize_x(0, 0, M)
+            if step in (2, 3, 4, 5):
+                clear_page(step - 2, ("tab1", "w1_bf01", "w1_bf11", "w3_bf0")[step - 2])
 
         tiles = [(b, t) for b in range(2) for t in range(PACK)]
-        to_pick, to_shift = None, None
+        to_pick = None
         for step, (b, t) in enumerate(tiles):
             h = ring.tile([P, S], F32, name="h", bufs=3)
             sums = [products(b, t, c) for c in range(2)]
-            squares = []
+            squares = [ring.tile([P, BANK], F32, name="sq", bufs=6) for c in range(2)]
+            if step == 0:
+                squares[1] = squares[0]
+            for c in range(2 if step else 1):
+                nc.scalar.activation(squares[c][:], sums[c][0][:], ACT.Square)
             for c in range(2):
-                sq = ring.tile([P, BANK], F32, name="sq", bufs=6)
-                nc.scalar.activation(sq[:], sums[c][0][:], ACT.Square)
-                squares.append(sq)
-            for c in range(2):
+                if step == 0 and c == 1:
+                    nc.scalar.activation(squares[c][:], sums[c][0][:], ACT.Square)
                 root = ring.tile([P, BANK], F32, name="root", bufs=5)
                 nc.scalar.activation(root[:], squares[c][:], ACT.Sqrt, bias=unit_t[:, b, t : t + 1])
                 nc.vector.tensor_tensor(h[:, BANK * c : BANK * (c + 1)], root[:], sums[c][1][:], ALU.subtract)
                 if c == 0 and to_pick is not None:
-                    pick(*to_pick, squares[0])
-            if to_shift is not None:
-                add_shift(*to_shift)
-            if to_pick is not None:
-                to_shift = (to_pick[0], to_pick[1], squares[0])
+                    pick(*to_pick, squares[0], 0, M)
             to_pick = (b, t, h)
             side_work(step)
         nc.scalar.activation(warm[:, 1:2], root[:, 0:1], ACT.Tanh)
-        add_shift(*to_shift)
-        pick(*to_pick, squares[1])
-        add_shift(to_pick[0], to_pick[1], squares[1])
-        x_q[1] = quantize(weave(1), "x1")
+        halves = ((0, M // 2), (M // 2, M))
+        for lo, hi in halves:
+            pick(*to_pick, squares[1], lo, hi)
+        for lo, hi in halves:
+            weave(nc.vector.tensor_copy, 1, lo, hi)
+            quantize_x(1, lo, hi)
         wgo_t = load("wgo_t", [P, M], F32, wgo, "w2_then_wgo")
         clim = load_rows("clim", climate)
 
         out_rows = out.rearrange("(p i) c -> p i c", i=PACK)
 
-        def place(i, y):
-            nc.vector.tensor_tensor(pages[i][:].indirect(idx3[:]), y[:], wgo_t[:], ALU.mult)
-            nc.sync.dma_start(out_rows[:, i, :], pages[i][:])
+        def place(i, lo, hi, y):
+            nc.vector.tensor_tensor(
+                pages[i][:].indirect(idx3[:, lo // 16 : hi // 16]), y[:, lo:hi], wgo_t[:, lo:hi], ALU.mult
+            )
+            if hi == M:
+                nc.sync.dma_start(out_rows[:, i, :], pages[i][:])
 
         to_place = None
-        for i in range(PACK):
+        for i, lo, hi in [(0, *half) for half in halves] + [(i, 0, M) for i in range(1, PACK)]:
             rows = slice(P * i, P * (i + 1))
             need = psum.tile([P, M], F32, name="clean", bufs=5)
             for b in range(2):
                 nc.tensor.matmul_mx(
-                    out=need[:],
+                    out=need[:, lo:hi],
                     lhsT=w3_q[b][0][:, rows].bitcast(FP8X4),
                     lhsT_scale=w3_q[b][1][:, rows],
-                    rhs=x_q[b][0][:].bitcast(FP8X4),
-                    rhs_scale=x_q[b][1][:],
+                    rhs=x_q[b][0][:, lo:hi].bitcast(FP8X4),
+                    rhs_scale=x_q[b][1][:, lo:hi],
                     start=(b == 0),
                     stop=(b == 1),
                 )
-            score = ring.tile([P, M], F32, name="score", bufs=4)
-            nc.scalar.activation(score[:], need[:], ACT.Tanh, scale=sens_t[:, i : i + 1])
-            y = ring.tile([P, M], F32, name="y", bufs=4)
-            nc.vector.tensor_tensor(y[:], score[:], clim[:, i, :], ALU.add)
+            score = ring.tile([P, M], F32, name="score", bufs=5)
+            nc.scalar.activation(score[:, lo:hi], need[:, lo:hi], ACT.Tanh, scale=sens_t[:, i : i + 1])
+            y = ring.tile([P, M], F32, name="y", bufs=5)
+            nc.vector.tensor_tensor(y[:, lo:hi], score[:, lo:hi], clim[:, i, lo:hi], ALU.add)
             if to_place is not None:
                 place(*to_place)
-            to_place = (i, y)
+            to_place = (i, lo, hi, y)
         place(*to_place)

@@ -1,6 +1,7 @@
 from contextlib import ExitStack
 
 import concourse.mybir as mybir
+from concourse.masks import make_identity
 
 K, H, N, T, S, M, T2 = 1024, 1024, 512, 2048, 1024, 512, 1024
 FLOPS = 2 * (2 * K * H * S + H * N * M)
@@ -20,7 +21,11 @@ P = 128
 PACK = 4
 PASS = P * PACK
 BANK = 512
-SHIFTED = 112
+PER_COLUMN = 16
+QUADRANT = 32
+MOVED = 112
+W1_STEPS = [1, 2]
+SLICES_ADDED_ON_VECTOR = 2
 
 
 def tile_list_pane_treatment_need_kernel(
@@ -30,94 +35,96 @@ def tile_list_pane_treatment_need_kernel(
     with ExitStack() as ctx:
         keep = ctx.enter_context(tc.tile_pool(name="keep", bufs=1))
         ring = ctx.enter_context(tc.tile_pool(name="ring", bufs=2))
-        psum = ctx.enter_context(tc.psum_pool(name="psum", bufs=4))
+        psum = ctx.enter_context(tc.psum_pool(name="psum", bufs=1))
 
-        def held(name, shape, dtype, tag=None):
-            return keep.tile(shape, dtype, name=name, tag=tag or name, align_bytes=64)
+        def held(name, shape, dtype, after=None):
+            return keep.tile(shape, dtype, name=name, tag=after or name, align_bytes=64)
 
-        tab_sc = keep.tile([P, T], U8, name="tab_sc", tag="tab_sc", align_bytes=64)
-        w2_sc_raw = held("w2_sc_raw", [P, H], U8)
-        nc.gpsimd.memset(w2_sc_raw[:].bitcast(I32), 0)
-        nc.gpsimd.memset(tab_sc[:].bitcast(I32), 0)
-        v_sc1 = held("v_sc1", [P, S], U8)
-        w2_sc1 = held("w2_sc1", [P, H], U8)
-        for plane in (v_sc1, w2_sc1):
-            nc.vector.memset(plane[:].bitcast(I32), 0)
+        def short_bank():
+            return psum.tile([P, BANK], F32, name="short", bufs=3)
+
+        def long_bank():
+            return psum.tile([P, BANK], F32, name="long", bufs=5)
+
         one = held("one", [P, 1], F32)
         nc.vector.memset(one[:], 1.0)
-        warm = held("warm", [P, 2], F32)
+        tab_planes = held("tab_planes", [P, T], U8)
+        w2_planes_raw = held("w2_planes_raw", [P, H], U8)
+        nc.vector.memset(tab_planes[:].bitcast(I32), 0)
+        nc.gpsimd.memset(w2_planes_raw[:].bitcast(I32), 0)
+        v_plane1 = held("v_plane1", [P, S], U8)
+        w2_plane1 = held("w2_plane1", [P, H], U8)
+        for plane in (v_plane1, w2_plane1):
+            nc.vector.memset(plane[:].bitcast(I32), 0)
+        pages = [held("page%d" % i, [P, T2], F32) for i in range(PACK)]
+        for page in pages:
+            nc.vector.memset(page[:], 0.0)
 
-        def load(name, shape, dtype, src, tag=None, bufs=1):
-            t = keep.tile(shape, dtype, name=name, tag=tag or name, bufs=bufs, align_bytes=64)
-            nc.sync.dma_start(t[:], src)
-            return t
+        for queue, planes, scales in ((nc.scalar, tab_planes, tab_scales), (nc.gpsimd, w2_planes_raw, w2_scales)):
+            for q in range(P // QUADRANT):
+                queue.dma_start(
+                    planes[QUADRANT * q : QUADRANT * q + 8, :].bitcast(I32), scales.bitcast(I32)[:, 4 * q : 4 * q + 4, :]
+                )
+        warm_sqrt = held("warm_sqrt", [P, 1], F32)
+        nc.scalar.activation(warm_sqrt[:], one[:], ACT.Sqrt)
+        unit_t = held("unit_t", [P, 2, PACK], F32)
+        shift_t = held("shift_t", [P, 2, PACK], F32)
+        sens_t = held("sens_t", [P, PACK], F32)
+        nc.gpsimd.dma_start(unit_t[:], unit.rearrange("(b p t) -> p b t", p=P, t=PACK))
+        nc.gpsimd.dma_start(shift_t[:], shift.rearrange("(b p t) -> p b t", p=P, t=PACK))
+        nc.gpsimd.dma_start(sens_t[:], sens.rearrange("(p t) -> p t", t=PACK))
 
-        def load_rows(name, rows):
-            return load(name, [P, PACK, PASS], F32, rows.rearrange("(p j) c -> p j c", j=PACK), "rows", 2)
+        def load(name, shape, dtype, src, after=None):
+            loaded = held(name, shape, dtype, after)
+            nc.sync.dma_start(loaded[:], src)
+            return loaded
 
-        def load_w2(b):
-            words = w2_words.bitcast(I32)[:, :, 256 * b : 256 * (b + 1)]
-            return load("w2_raw%d" % b, [P, 2, 256], I32, words.rearrange("a p c -> p a c"), "w2_then_wgo")
+        def load_rows(name, rows, after=None):
+            return load(name, [P, PACK, PASS], F32, rows.rearrange("(p j) c -> p j c", j=PACK), after)
 
-        for q in range(4):
-            nc.gpsimd.dma_start(
-                tab_sc[32 * q : 32 * q + 8, :].bitcast(I32), tab_scales.bitcast(I32)[:, 4 * q : 4 * q + 4, :]
-            )
-        for q in range(4):
-            nc.scalar.dma_start(
-                w2_sc_raw[32 * q : 32 * q + 8, :].bitcast(I32), w2_scales.bitcast(I32)[:, 4 * q : 4 * q + 4, :]
-            )
-        nc.scalar.activation(warm[:, 0:1], one[:], ACT.Sqrt)
+        def load_tab(a, after=None):
+            return load("tab%d" % a, [P, T], I32, tab_words[a].rearrange("p t i -> p (t i)").bitcast(I32), after)
 
-        idx = load("idx", [P, S // 16], U16, offs)
-        def load_tab(a):
-            return load("tab%d" % a, [P, T], I32, tab_words[a].rearrange("p t i -> p (t i)").bitcast(I32))
+        def load_w1(a, b, after=None):
+            return load_rows("w1_raw%d%d" % (a, b), w1[PASS * a : PASS * (a + 1), PASS * b : PASS * (b + 1)], after)
 
-        def load_w1(a, b):
-            return load_rows("w1_raw%d%d" % (a, b), w1[PASS * a : PASS * (a + 1), PASS * b : PASS * (b + 1)])
+        def load_w2(b, after=None):
+            pairs = w2_words.bitcast(I32)[:, :, PASS // 2 * b : PASS // 2 * (b + 1)]
+            return load("w2_raw%d" % b, [P, 2, PASS // 2], I32, pairs.rearrange("a p c -> p a c"), after)
 
-        tab, w1_raw, w2_raw = {}, {}, {}
+        tab, w1_raw, w2_raw, w3_raw = {}, {}, {}, {}
+        idx = load("idx", [P, S // PER_COLUMN], U16, offs)
+        idx2 = load("idx2", [P, M // PER_COLUMN], U16, offs2)
         tab[0] = load_tab(0)
         w1_raw[0, 0] = load_w1(0, 0)
         w2_raw[0] = load_w2(0)
-        w1_raw[1, 0] = load_w1(1, 0)
-        tab[1] = load_tab(1)
-        unit_t = load("unit_t", [P, 2, PACK], F32, unit.rearrange("(b p i) -> p b i", p=P, i=PACK))
-        idx2 = load("idx2", [P, M // 16], U16, offs2)
-        shift_t = load("shift_t", [P, 2, PACK], F32, shift.rearrange("(b p i) -> p b i", p=P, i=PACK))
-        idx3 = load("idx3", [P, M // 16], U16, offs3)
-        sens_t = load("sens_t", [P, PACK], F32, sens.rearrange("(p i) -> p i", i=PACK))
+        w1_raw[1, 0] = load_w1(1, 0, "one")
+        tab[1] = load_tab(1, "warm_sqrt")
+        idx3 = load("idx3", [P, M // PER_COLUMN], U16, offs3)
+
+        def entries(index_tile, lo, hi):
+            return index_tile[:, lo // PER_COLUMN : hi // PER_COLUMN]
 
         v_words = {}
-        v_sc = held("v_sc", [P, S], U8)
 
-        def gather_words(a, c, tag=None):
-            v_words[a, c] = held("v%d%d" % (a, c), [P, BANK], U32, tag)
-            nc.vector.tensor_copy(v_words[a, c][:], tab[a][:].bitcast(U32).indirect(idx[:, 32 * c : 32 * (c + 1)]))
+        def gather_words(a, c, after=None):
+            v_words[a, c] = held("v_words%d%d" % (a, c), [P, BANK], U32, after)
+            nc.vector.tensor_copy(v_words[a, c][:], tab[a][:].bitcast(U32).indirect(entries(idx, BANK * c, BANK * (c + 1))))
 
-        gather_words(0, 0)
-        gather_words(0, 1)
-        nc.vector.tensor_copy(v_sc[:], tab_sc[:].indirect(idx[:]))
-        nc.sync.dma_start(v_sc1[0:SHIFTED, :].bitcast(I32), v_sc[4 : 4 + SHIFTED, :].bitcast(I32))
+        def move_up(plane1, planes):
+            nc.sync.dma_start(plane1[0:MOVED, :].bitcast(I32), planes[4 : 4 + MOVED, :].bitcast(I32))
 
-        w2_sc = held("w2_sc", [P, H], U8, "tab0")
-        nc.vector.tensor_copy(
-            w2_sc[:].rearrange("p (b t m) -> p b m t", b=2, t=PACK),
-            w2_sc_raw[:].rearrange("p (b m t) -> p b m t", b=2, t=PACK),
-        )
-        nc.sync.dma_start(w2_sc1[0:SHIFTED, :].bitcast(I32), w2_sc[4 : 4 + SHIFTED, :].bitcast(I32))
-
-        def cast(copy, grouped, raw, lo, hi):
-            dst = grouped[:].rearrange("p (t m j) -> p m j t", t=PACK, j=PACK)
+        def round_weight(grouped, raw, t_range):
+            dst = grouped[:].rearrange("p (t m j) -> p m j t", m=P, j=PACK)
             src = raw[:].rearrange("p j (m t) -> p m j t", t=PACK)
-            copy(dst[:, lo:hi], src[:, lo:hi])
+            nc.scalar.copy(dst, src[:, :, :, t_range])
 
-        def quantize(grouped, name, tag=None):
+        def quantize(grouped, name):
             width = grouped.shape[1] // PACK
-            codes = held(name + "_codes", [P, width], U32, tag)
-            scales = held(name + "_scales", [P, width], U8)
-            nc.vector.quantize_mx(out=codes[:].bitcast(FP8X4), scales=scales[:], in_=grouped[:])
-            return codes, scales
+            codes = held(name + "_codes", [P, width], U32)
+            plane = held(name + "_plane", [P, width], U8)
+            nc.vector.quantize_mx(out=codes[:].bitcast(FP8X4), scales=plane[:], in_=grouped[:])
+            return codes, plane
 
         def deal_w2(b):
             dealt = held("w2_dealt%d" % b, [P, 2, 2 * PASS], U8)
@@ -127,64 +134,74 @@ def tile_list_pane_treatment_need_kernel(
             )
             return dealt
 
-        w1_bf = {(a, b): held("w1_bf%d%d" % (a, b), [P, PASS * PACK], BF16) for a in range(2) for b in range(2)}
-        w3_bf = [held("w3_bf%d" % b, [P, PASS * PACK], BF16) for b in range(2)]
-        w1_q, w2_q, w3_q, w3_raw = {}, {}, {}, {}
-        for a in range(2):
-            cast(nc.scalar.copy, w1_bf[a, 0], w1_raw[a, 0], 0, P)
-        w1_q[0, 0] = quantize(w1_bf[0, 0], "w1_00", "tab_sc")
-        wgt_t = load("wgt_t", [P, M], F32, wgt, "w1_bf00")
+        gather_words(0, 0)
+        gather_words(0, 1)
+        wgt_t = load("wgt_t", [P, M], F32, wgt, "tab0")
+        v_planes = held("v_planes", [P, S], U8)
+        nc.vector.tensor_copy(v_planes[:], tab_planes[:].indirect(idx[:]))
+        move_up(v_plane1, v_planes)
+        w2_planes = held("w2_planes", [P, H], U8, "tab_planes")
+        nc.vector.tensor_copy(
+            w2_planes[:].rearrange("p (b t m) -> p b m t", b=2, t=PACK),
+            w2_planes_raw[:].rearrange("p (b m t) -> p b m t", b=2, t=PACK),
+        )
+        move_up(w2_plane1, w2_planes)
+
+        w1_q, w2_q, w3_q = {}, {}, {}
+
+        def quantize_w1(a, b, after=None):
+            name = "w1_%d%d" % (a, b)
+            grouped = held(name, [P, PASS * PACK], BF16, after)
+            round_weight(grouped, w1_raw[a, b], slice(0, PACK))
+            w1_q[a, b] = quantize(grouped, name)
+
+        quantize_w1(0, 0)
         w2_q[0] = deal_w2(0)
-        w1_q[1, 0] = quantize(w1_bf[1, 0], "w1_10")
-        gather_words(1, 0, "w1_bf10")
+        quantize_w1(1, 0)
+        gather_words(1, 0, "w1_10")
         gather_words(1, 1)
-        for a in range(2):
-            w1_raw[a, 1] = load_w1(a, 1)
-        w2_raw[1] = load_w2(1)
+        w1_raw[0, 1] = load_w1(0, 1, "w2_planes_raw")
+        w1_raw[1, 1] = load_w1(1, 1, "one")
+        w2_raw[1] = load_w2(1, "w2_raw0")
 
         def products(b, t, c):
             rows = slice(P * t, P * (t + 1))
             cols = slice(BANK * c, BANK * (c + 1))
-            trace = psum.tile([P, BANK], F32, name="trace", bufs=3)
+            trace = short_bank()
             for a in range(2):
-                codes, scales = w1_q[a, b]
+                codes, plane = w1_q[a, b]
                 nc.tensor.matmul_mx(
                     out=trace[:],
                     lhsT=codes[:, rows].bitcast(FP8X4),
-                    lhsT_scale=scales[:, rows],
+                    lhsT_scale=plane[:, rows],
                     rhs=v_words[a, c][:].bitcast(FP8X4),
-                    rhs_scale=v_sc[4 * a : P, cols],
+                    rhs_scale=v_planes[4 * a : P, cols],
                     start=(a == 0),
                     stop=(a == 1),
                 )
-            clean = psum.tile([P, BANK], F32, name="clean", bufs=5)
+            clean = long_bank()
             for a in range(2):
                 nc.tensor.matmul_mx(
                     out=clean[:],
                     lhsT=w2_q[b][:, a, 2 * P * t : 2 * P * (t + 1)].bitcast(FP4X4),
-                    lhsT_scale=(w2_sc, w2_sc1)[a][:, PASS * b + P * t : PASS * b + P * (t + 1)],
+                    lhsT_scale=(w2_planes, w2_plane1)[a][:, PASS * b + P * t : PASS * b + P * (t + 1)],
                     rhs=v_words[a, c][:].bitcast(FP8X4),
-                    rhs_scale=(v_sc, v_sc1)[a][:, cols],
+                    rhs_scale=(v_planes, v_plane1)[a][:, cols],
                     start=(a == 0),
                     stop=(a == 1),
                 )
             return trace, clean
 
         x_rows = [held("x_rows%d" % b, [P, PACK, M], BF16) for b in range(2)]
+        x_bf = [held("x_bf%d" % b, [P, M * PACK], BF16) for b in range(2)]
+        x_q = [(held("x_codes%d" % b, [P, M], U32), held("x_plane%d" % b, [P, M], U8)) for b in range(2)]
+        list_halves = ((0, M // 2), (M // 2, M))
 
         def pick(b, t, h, picked, lo, hi):
-            nc.vector.tensor_tensor(
-                picked[:, lo:hi], h[:].indirect(idx2[:, lo // 16 : hi // 16]), wgt_t[:, lo:hi], ALU.mult
-            )
-            add_shift(b, t, picked, lo, hi)
-
-        def add_shift(b, t, picked, lo, hi):
+            nc.vector.tensor_tensor(picked[:, lo:hi], h[:].indirect(entries(idx2, lo, hi)), wgt_t[:, lo:hi], ALU.mult)
             nc.gpsimd.tensor_scalar(
                 x_rows[b][:, t, lo:hi], picked[:, lo:hi], 1.0, shift_t[:, b, t : t + 1], ALU.mult, ALU.add
             )
-
-        x_bf = [held("x_bf%d" % b, [P, M * PACK], BF16) for b in range(2)]
-        x_q = [(held("x_codes%d" % b, [P, M], U32), held("x_scales%d" % b, [P, M], U8)) for b in range(2)]
 
         def weave(copy, b, lo, hi):
             copy(
@@ -193,94 +210,115 @@ def tile_list_pane_treatment_need_kernel(
             )
 
         def quantize_x(b, lo, hi):
+            codes, plane = x_q[b]
             nc.vector.quantize_mx(
-                out=x_q[b][0][:, lo:hi].bitcast(FP8X4), scales=x_q[b][1][:, lo:hi], in_=x_bf[b][:, PACK * lo : PACK * hi]
+                out=codes[:, lo:hi].bitcast(FP8X4), scales=plane[:, lo:hi], in_=x_bf[b][:, PACK * lo : PACK * hi]
             )
 
-        pages = {}
-
-        def clear_page(i, tag):
-            pages[i] = held("page%d" % i, [P, T2], F32, tag)
-            nc.gpsimd.memset(pages[i][:], 0.0)
+        def quantize_w3(b, half):
+            name = "w3_%d%d" % (b, half)
+            grouped = held(name, [P, PASS * PACK // 2], BF16)
+            round_weight(grouped, w3_raw[b], slice(2 * half, 2 * half + 2))
+            w3_q[b, half] = quantize(grouped, name)
 
         def side_work(step):
-            half = P // 2
-            if step < 2:
-                cast(nc.scalar.copy, w1_bf[step, 1], w1_raw[step, 1], 0, P)
-                w1_q[step, 1] = quantize(w1_bf[step, 1], "w1_%d1" % step)
-                w3_raw[step] = load_rows("w3_raw%d" % step, w3[PASS * step : PASS * (step + 1), :])
-            if step == 2:
+            if step == 0:
                 w2_q[1] = deal_w2(1)
-            if step in (3, 4, 5, 6):
-                b, part = divmod(step - 3, 2)
-                cast(nc.scalar.copy, w3_bf[b], w3_raw[b], half * part, half * (part + 1))
-                if part == 1:
-                    w3_q[b] = quantize(w3_bf[b], "w3_%d" % b)
+            if step in W1_STEPS:
+                a = W1_STEPS.index(step)
+                quantize_w1(a, 1, "square_before_w1_%d1" % a)
+                w3_raw[a] = load_rows("w3_raw%d" % a, w3[PASS * a : PASS * (a + 1), :], ("w2_planes_raw", "one")[a])
+            if step in (3, 4):
+                quantize_w3(step - 3, 0)
             if step == 5:
-                weave(nc.scalar.copy, 0, 0, M // 2)
-                weave(nc.vector.tensor_copy, 0, M // 2, M)
+                weave(nc.scalar.copy, 0, *list_halves[0])
+                weave(nc.vector.tensor_copy, 0, *list_halves[1])
             if step == 6:
                 quantize_x(0, 0, M)
-            if step in (2, 3, 4, 5):
-                clear_page(step - 2, ("tab1", "w1_bf01", "w1_bf11", "w3_bf0")[step - 2])
 
-        tiles = [(b, t) for b in range(2) for t in range(PACK)]
         to_pick = None
-        for step, (b, t) in enumerate(tiles):
+        for step in range(2 * PACK):
+            b, t = divmod(step, PACK)
             h = ring.tile([P, S], F32, name="h", bufs=3)
             sums = [products(b, t, c) for c in range(2)]
-            squares = [ring.tile([P, BANK], F32, name="sq", bufs=6) for c in range(2)]
-            if step == 0:
-                squares[1] = squares[0]
-            for c in range(2 if step else 1):
-                nc.scalar.activation(squares[c][:], sums[c][0][:], ACT.Square)
-            for c in range(2):
-                if step == 0 and c == 1:
+            squares = [ring.tile([P, BANK], F32, name="square", bufs=6)]
+            if step in W1_STEPS:
+                squares.append(held("square_before_w1_%d1" % W1_STEPS.index(step), [P, BANK], F32))
+            elif step:
+                squares.append(ring.tile([P, BANK], F32, name="square", bufs=6))
+            if step:
+                for c in range(2):
                     nc.scalar.activation(squares[c][:], sums[c][0][:], ACT.Square)
+            for c in range(2):
+                if not step:
+                    nc.scalar.activation(squares[0][:], sums[c][0][:], ACT.Square)
                 root = ring.tile([P, BANK], F32, name="root", bufs=5)
-                nc.scalar.activation(root[:], squares[c][:], ACT.Sqrt, bias=unit_t[:, b, t : t + 1])
+                nc.scalar.activation(root[:], squares[c if step else 0][:], ACT.Sqrt, bias=unit_t[:, b, t : t + 1])
                 nc.vector.tensor_tensor(h[:, BANK * c : BANK * (c + 1)], root[:], sums[c][1][:], ALU.subtract)
                 if c == 0 and to_pick is not None:
                     pick(*to_pick, squares[0], 0, M)
             to_pick = (b, t, h)
             side_work(step)
-        nc.scalar.activation(warm[:, 1:2], root[:, 0:1], ACT.Tanh)
-        halves = ((0, M // 2), (M // 2, M))
-        for lo, hi in halves:
+
+        warm_tanh = held("warm_tanh", [P, 1], F32)
+        nc.scalar.activation(warm_tanh[:], root[:, 0:1], ACT.Tanh)
+        for lo, hi in list_halves:
             pick(*to_pick, squares[1], lo, hi)
-        for lo, hi in halves:
+        for lo, hi in list_halves:
             weave(nc.vector.tensor_copy, 1, lo, hi)
             quantize_x(1, lo, hi)
-        wgo_t = load("wgo_t", [P, M], F32, wgo, "w2_then_wgo")
-        clim = load_rows("clim", climate)
+        for b in range(2):
+            quantize_w3(b, 1)
+        wgo_t = load("wgo_t", [P, M], F32, wgo, "w2_raw0")
+        climate_t = load_rows("climate_t", climate, "square_before_w1_11")
+        ident = held("ident", [P, P], F32, "square_before_w1_01")
+        make_identity(nc, ident[:])
 
         out_rows = out.rearrange("(p i) c -> p i c", i=PACK)
+        blocks = [slice(P * j, P * (j + 1)) for j in range(M // P)]
+
+        def add_climate(i, lo, hi, score):
+            if i < SLICES_ADDED_ON_VECTOR:
+                y = held("y%d_%d" % (i, lo), [P, M], F32, "w3_11" if i == 1 else None)
+                nc.vector.tensor_tensor(y[:, lo:hi], score[:, lo:hi], climate_t[:, i, lo:hi], ALU.add)
+                return y
+            turned = short_bank()
+            for blk in blocks:
+                nc.tensor.matmul(turned[:, blk], score[:, blk], ident[:], start=True, stop=False, is_transpose=True)
+                nc.tensor.matmul(turned[:, blk], climate_t[:, i, blk], ident[:], start=False, stop=True, is_transpose=True)
+            y_turned = ring.tile([P, M], F32, name="y_turned")
+            nc.scalar.copy(y_turned[:], turned[:])
+            back = short_bank()
+            for blk in blocks:
+                nc.tensor.transpose(back[:, blk], y_turned[:, blk], ident[:])
+            y = held("y%d_%d" % (i, lo), [P, M], F32)
+            nc.scalar.copy(y[:], back[:])
+            return y
 
         def place(i, lo, hi, y):
-            nc.vector.tensor_tensor(
-                pages[i][:].indirect(idx3[:, lo // 16 : hi // 16]), y[:, lo:hi], wgo_t[:, lo:hi], ALU.mult
-            )
+            nc.vector.tensor_tensor(pages[i][:].indirect(entries(idx3, lo, hi)), y[:, lo:hi], wgo_t[:, lo:hi], ALU.mult)
             if hi == M:
                 nc.sync.dma_start(out_rows[:, i, :], pages[i][:])
 
         to_place = None
-        for i, lo, hi in [(0, *half) for half in halves] + [(i, 0, M) for i in range(1, PACK)]:
-            rows = slice(P * i, P * (i + 1))
-            need = psum.tile([P, M], F32, name="clean", bufs=5)
+        for i, lo, hi in [(0, *half) for half in list_halves] + [(i, 0, M) for i in range(1, PACK)]:
+            half, within = divmod(i, PACK // 2)
+            rows = slice(P * within, P * (within + 1))
+            need = long_bank()
             for b in range(2):
+                codes, plane = w3_q[b, half]
                 nc.tensor.matmul_mx(
                     out=need[:, lo:hi],
-                    lhsT=w3_q[b][0][:, rows].bitcast(FP8X4),
-                    lhsT_scale=w3_q[b][1][:, rows],
+                    lhsT=codes[:, rows].bitcast(FP8X4),
+                    lhsT_scale=plane[:, rows],
                     rhs=x_q[b][0][:, lo:hi].bitcast(FP8X4),
                     rhs_scale=x_q[b][1][:, lo:hi],
                     start=(b == 0),
                     stop=(b == 1),
                 )
-            score = ring.tile([P, M], F32, name="score", bufs=5)
+            score = held("score%d_%d" % (i, lo), [P, M], F32)
             nc.scalar.activation(score[:, lo:hi], need[:, lo:hi], ACT.Tanh, scale=sens_t[:, i : i + 1])
-            y = ring.tile([P, M], F32, name="y", bufs=5)
-            nc.vector.tensor_tensor(y[:, lo:hi], score[:, lo:hi], clim[:, i, lo:hi], ALU.add)
+            y = add_climate(i, lo, hi, score)
             if to_place is not None:
                 place(*to_place)
             to_place = (i, lo, hi, y)

from contextlib import ExitStack

import concourse.mybir as mybir
from concourse.masks import make_identity

K, H, N, T, S, M, T2 = 1024, 1024, 512, 2048, 1024, 512, 1024
FLOPS = 2 * (2 * K * H * S + H * N * M)

F32 = mybir.dt.float32
BF16 = mybir.dt.bfloat16
I32 = mybir.dt.int32
U32 = mybir.dt.uint32
U16 = mybir.dt.uint16
U8 = mybir.dt.uint8
FP8X4 = mybir.dt.float8_e4m3fn_x4
FP4X4 = mybir.dt.float4_e2m1fn_x4
ALU = mybir.AluOpType
ACT = mybir.ActivationFunctionType

P = 128
PACK = 4
PASS = P * PACK
BANK = 512
PER_COLUMN = 16
QUADRANT = 32
MOVED = 112
W1_STEPS = [1, 2]
SLICES_ADDED_ON_VECTOR = 2


def tile_list_pane_treatment_need_kernel(
    tc, tab_words, tab_scales, offs, w1, w2_words, w2_scales, unit, offs2, wgt, shift, w3, sens, climate, offs3, wgo, out
):
    nc = tc.nc
    with ExitStack() as ctx:
        keep = ctx.enter_context(tc.tile_pool(name="keep", bufs=1))
        ring = ctx.enter_context(tc.tile_pool(name="ring", bufs=2))
        psum = ctx.enter_context(tc.psum_pool(name="psum", bufs=1))

        def held(name, shape, dtype, after=None):
            return keep.tile(shape, dtype, name=name, tag=after or name, align_bytes=64)

        def short_bank():
            return psum.tile([P, BANK], F32, name="short", bufs=3)

        def long_bank():
            return psum.tile([P, BANK], F32, name="long", bufs=5)

        one = held("one", [P, 1], F32)
        nc.vector.memset(one[:], 1.0)
        tab_planes = held("tab_planes", [P, T], U8)
        w2_planes_raw = held("w2_planes_raw", [P, H], U8)
        nc.vector.memset(tab_planes[:].bitcast(I32), 0)
        nc.gpsimd.memset(w2_planes_raw[:].bitcast(I32), 0)
        v_plane1 = held("v_plane1", [P, S], U8)
        w2_plane1 = held("w2_plane1", [P, H], U8)
        for plane in (v_plane1, w2_plane1):
            nc.vector.memset(plane[:].bitcast(I32), 0)
        pages = [held("page%d" % i, [P, T2], F32) for i in range(PACK)]
        for page in pages:
            nc.vector.memset(page[:], 0.0)

        for queue, planes, scales in ((nc.scalar, tab_planes, tab_scales), (nc.gpsimd, w2_planes_raw, w2_scales)):
            for q in range(P // QUADRANT):
                queue.dma_start(
                    planes[QUADRANT * q : QUADRANT * q + 8, :].bitcast(I32), scales.bitcast(I32)[:, 4 * q : 4 * q + 4, :]
                )
        warm_sqrt = held("warm_sqrt", [P, 1], F32)
        nc.scalar.activation(warm_sqrt[:], one[:], ACT.Sqrt)
        unit_t = held("unit_t", [P, 2, PACK], F32)
        shift_t = held("shift_t", [P, 2, PACK], F32)
        sens_t = held("sens_t", [P, PACK], F32)
        nc.gpsimd.dma_start(unit_t[:], unit.rearrange("(b p t) -> p b t", p=P, t=PACK))
        nc.gpsimd.dma_start(shift_t[:], shift.rearrange("(b p t) -> p b t", p=P, t=PACK))
        nc.gpsimd.dma_start(sens_t[:], sens.rearrange("(p t) -> p t", t=PACK))

        def load(name, shape, dtype, src, after=None):
            loaded = held(name, shape, dtype, after)
            nc.sync.dma_start(loaded[:], src)
            return loaded

        def load_rows(name, rows, after=None):
            return load(name, [P, PACK, PASS], F32, rows.rearrange("(p j) c -> p j c", j=PACK), after)

        def load_tab(a, after=None):
            return load("tab%d" % a, [P, T], I32, tab_words[a].rearrange("p t i -> p (t i)").bitcast(I32), after)

        def load_w1(a, b, after=None):
            return load_rows("w1_raw%d%d" % (a, b), w1[PASS * a : PASS * (a + 1), PASS * b : PASS * (b + 1)], after)

        def load_w2(b, after=None):
            pairs = w2_words.bitcast(I32)[:, :, PASS // 2 * b : PASS // 2 * (b + 1)]
            return load("w2_raw%d" % b, [P, 2, PASS // 2], I32, pairs.rearrange("a p c -> p a c"), after)

        tab, w1_raw, w2_raw, w3_raw = {}, {}, {}, {}
        idx = load("idx", [P, S // PER_COLUMN], U16, offs)
        idx2 = load("idx2", [P, M // PER_COLUMN], U16, offs2)
        tab[0] = load_tab(0)
        w1_raw[0, 0] = load_w1(0, 0)
        w2_raw[0] = load_w2(0)
        w1_raw[1, 0] = load_w1(1, 0, "one")
        tab[1] = load_tab(1, "warm_sqrt")
        idx3 = load("idx3", [P, M // PER_COLUMN], U16, offs3)

        def entries(index_tile, lo, hi):
            return index_tile[:, lo // PER_COLUMN : hi // PER_COLUMN]

        v_words = {}

        def gather_words(a, c, after=None):
            v_words[a, c] = held("v_words%d%d" % (a, c), [P, BANK], U32, after)
            nc.vector.tensor_copy(v_words[a, c][:], tab[a][:].bitcast(U32).indirect(entries(idx, BANK * c, BANK * (c + 1))))

        def move_up(plane1, planes):
            nc.sync.dma_start(plane1[0:MOVED, :].bitcast(I32), planes[4 : 4 + MOVED, :].bitcast(I32))

        def round_weight(grouped, raw, t_range):
            dst = grouped[:].rearrange("p (t m j) -> p m j t", m=P, j=PACK)
            src = raw[:].rearrange("p j (m t) -> p m j t", t=PACK)
            nc.scalar.copy(dst, src[:, :, :, t_range])

        def quantize(grouped, name):
            width = grouped.shape[1] // PACK
            codes = held(name + "_codes", [P, width], U32)
            plane = held(name + "_plane", [P, width], U8)
            nc.vector.quantize_mx(out=codes[:].bitcast(FP8X4), scales=plane[:], in_=grouped[:])
            return codes, plane

        def deal_w2(b):
            dealt = held("w2_dealt%d" % b, [P, 2, 2 * PASS], U8)
            nc.vector.tensor_copy(
                dealt[:].bitcast(U16).rearrange("p a (t m) -> p a m t", t=PACK),
                w2_raw[b][:].bitcast(U16).rearrange("p a (m t) -> p a m t", t=PACK),
            )
            return dealt

        gather_words(0, 0)
        gather_words(0, 1)
        wgt_t = load("wgt_t", [P, M], F32, wgt, "tab0")
        v_planes = held("v_planes", [P, S], U8)
        nc.vector.tensor_copy(v_planes[:], tab_planes[:].indirect(idx[:]))
        move_up(v_plane1, v_planes)
        w2_planes = held("w2_planes", [P, H], U8, "tab_planes")
        nc.vector.tensor_copy(
            w2_planes[:].rearrange("p (b t m) -> p b m t", b=2, t=PACK),
            w2_planes_raw[:].rearrange("p (b m t) -> p b m t", b=2, t=PACK),
        )
        move_up(w2_plane1, w2_planes)

        w1_q, w2_q, w3_q = {}, {}, {}

        def quantize_w1(a, b, after=None):
            name = "w1_%d%d" % (a, b)
            grouped = held(name, [P, PASS * PACK], BF16, after)
            round_weight(grouped, w1_raw[a, b], slice(0, PACK))
            w1_q[a, b] = quantize(grouped, name)

        quantize_w1(0, 0)
        w2_q[0] = deal_w2(0)
        quantize_w1(1, 0)
        gather_words(1, 0, "w1_10")
        gather_words(1, 1)
        w1_raw[0, 1] = load_w1(0, 1, "w2_planes_raw")
        w1_raw[1, 1] = load_w1(1, 1, "one")
        w2_raw[1] = load_w2(1, "w2_raw0")

        def products(b, t, c):
            rows = slice(P * t, P * (t + 1))
            cols = slice(BANK * c, BANK * (c + 1))
            trace = short_bank()
            for a in range(2):
                codes, plane = w1_q[a, b]
                nc.tensor.matmul_mx(
                    out=trace[:],
                    lhsT=codes[:, rows].bitcast(FP8X4),
                    lhsT_scale=plane[:, rows],
                    rhs=v_words[a, c][:].bitcast(FP8X4),
                    rhs_scale=v_planes[4 * a : P, cols],
                    start=(a == 0),
                    stop=(a == 1),
                )
            clean = long_bank()
            for a in range(2):
                nc.tensor.matmul_mx(
                    out=clean[:],
                    lhsT=w2_q[b][:, a, 2 * P * t : 2 * P * (t + 1)].bitcast(FP4X4),
                    lhsT_scale=(w2_planes, w2_plane1)[a][:, PASS * b + P * t : PASS * b + P * (t + 1)],
                    rhs=v_words[a, c][:].bitcast(FP8X4),
                    rhs_scale=(v_planes, v_plane1)[a][:, cols],
                    start=(a == 0),
                    stop=(a == 1),
                )
            return trace, clean

        x_rows = [held("x_rows%d" % b, [P, PACK, M], BF16) for b in range(2)]
        x_bf = [held("x_bf%d" % b, [P, M * PACK], BF16) for b in range(2)]
        x_q = [(held("x_codes%d" % b, [P, M], U32), held("x_plane%d" % b, [P, M], U8)) for b in range(2)]
        list_halves = ((0, M // 2), (M // 2, M))

        def pick(b, t, h, picked, lo, hi):
            nc.vector.tensor_tensor(picked[:, lo:hi], h[:].indirect(entries(idx2, lo, hi)), wgt_t[:, lo:hi], ALU.mult)
            nc.gpsimd.tensor_scalar(
                x_rows[b][:, t, lo:hi], picked[:, lo:hi], 1.0, shift_t[:, b, t : t + 1], ALU.mult, ALU.add
            )

        def weave(copy, b, lo, hi):
            copy(
                x_bf[b][:, PACK * lo : PACK * hi].rearrange("p (c i t) -> p c t i", i=4, t=PACK),
                x_rows[b][:, :, lo:hi].rearrange("p t (c i) -> p c t i", i=4),
            )

        def quantize_x(b, lo, hi):
            codes, plane = x_q[b]
            nc.vector.quantize_mx(
                out=codes[:, lo:hi].bitcast(FP8X4), scales=plane[:, lo:hi], in_=x_bf[b][:, PACK * lo : PACK * hi]
            )

        def quantize_w3(b, half):
            name = "w3_%d%d" % (b, half)
            grouped = held(name, [P, PASS * PACK // 2], BF16)
            round_weight(grouped, w3_raw[b], slice(2 * half, 2 * half + 2))
            w3_q[b, half] = quantize(grouped, name)

        def side_work(step):
            if step == 0:
                w2_q[1] = deal_w2(1)
            if step in W1_STEPS:
                a = W1_STEPS.index(step)
                quantize_w1(a, 1, "square_before_w1_%d1" % a)
                w3_raw[a] = load_rows("w3_raw%d" % a, w3[PASS * a : PASS * (a + 1), :], ("w2_planes_raw", "one")[a])
            if step in (3, 4):
                quantize_w3(step - 3, 0)
            if step == 5:
                weave(nc.scalar.copy, 0, *list_halves[0])
                weave(nc.vector.tensor_copy, 0, *list_halves[1])
            if step == 6:
                quantize_x(0, 0, M)

        to_pick = None
        for step in range(2 * PACK):
            b, t = divmod(step, PACK)
            h = ring.tile([P, S], F32, name="h", bufs=3)
            sums = [products(b, t, c) for c in range(2)]
            squares = [ring.tile([P, BANK], F32, name="square", bufs=6)]
            if step in W1_STEPS:
                squares.append(held("square_before_w1_%d1" % W1_STEPS.index(step), [P, BANK], F32))
            elif step:
                squares.append(ring.tile([P, BANK], F32, name="square", bufs=6))
            if step:
                for c in range(2):
                    nc.scalar.activation(squares[c][:], sums[c][0][:], ACT.Square)
            for c in range(2):
                if not step:
                    nc.scalar.activation(squares[0][:], sums[c][0][:], ACT.Square)
                root = ring.tile([P, BANK], F32, name="root", bufs=5)
                nc.scalar.activation(root[:], squares[c if step else 0][:], ACT.Sqrt, bias=unit_t[:, b, t : t + 1])
                nc.vector.tensor_tensor(h[:, BANK * c : BANK * (c + 1)], root[:], sums[c][1][:], ALU.subtract)
                if c == 0 and to_pick is not None:
                    pick(*to_pick, squares[0], 0, M)
            to_pick = (b, t, h)
            side_work(step)

        warm_tanh = held("warm_tanh", [P, 1], F32)
        nc.scalar.activation(warm_tanh[:], root[:, 0:1], ACT.Tanh)
        for lo, hi in list_halves:
            pick(*to_pick, squares[1], lo, hi)
        for lo, hi in list_halves:
            weave(nc.vector.tensor_copy, 1, lo, hi)
            quantize_x(1, lo, hi)
        for b in range(2):
            quantize_w3(b, 1)
        wgo_t = load("wgo_t", [P, M], F32, wgo, "w2_raw0")
        climate_t = load_rows("climate_t", climate, "square_before_w1_11")
        ident = held("ident", [P, P], F32, "square_before_w1_01")
        make_identity(nc, ident[:])

        out_rows = out.rearrange("(p i) c -> p i c", i=PACK)
        blocks = [slice(P * j, P * (j + 1)) for j in range(M // P)]

        def add_climate(i, lo, hi, score):
            if i < SLICES_ADDED_ON_VECTOR:
                y = held("y%d_%d" % (i, lo), [P, M], F32, "w3_11" if i == 1 else None)
                nc.vector.tensor_tensor(y[:, lo:hi], score[:, lo:hi], climate_t[:, i, lo:hi], ALU.add)
                return y
            turned = short_bank()
            for blk in blocks:
                nc.tensor.matmul(turned[:, blk], score[:, blk], ident[:], start=True, stop=False, is_transpose=True)
                nc.tensor.matmul(turned[:, blk], climate_t[:, i, blk], ident[:], start=False, stop=True, is_transpose=True)
            y_turned = ring.tile([P, M], F32, name="y_turned")
            nc.scalar.copy(y_turned[:], turned[:])
            back = short_bank()
            for blk in blocks:
                nc.tensor.transpose(back[:, blk], y_turned[:, blk], ident[:])
            y = held("y%d_%d" % (i, lo), [P, M], F32)
            nc.scalar.copy(y[:], back[:])
            return y

        def place(i, lo, hi, y):
            nc.vector.tensor_tensor(pages[i][:].indirect(entries(idx3, lo, hi)), y[:, lo:hi], wgo_t[:, lo:hi], ALU.mult)
            if hi == M:
                nc.sync.dma_start(out_rows[:, i, :], pages[i][:])

        to_place = None
        for i, lo, hi in [(0, *half) for half in list_halves] + [(i, 0, M) for i in range(1, PACK)]:
            half, within = divmod(i, PACK // 2)
            rows = slice(P * within, P * (within + 1))
            need = long_bank()
            for b in range(2):
                codes, plane = w3_q[b, half]
                nc.tensor.matmul_mx(
                    out=need[:, lo:hi],
                    lhsT=codes[:, rows].bitcast(FP8X4),
                    lhsT_scale=plane[:, rows],
                    rhs=x_q[b][0][:, lo:hi].bitcast(FP8X4),
                    rhs_scale=x_q[b][1][:, lo:hi],
                    start=(b == 0),
                    stop=(b == 1),
                )
            score = held("score%d_%d" % (i, lo), [P, M], F32)
            nc.scalar.activation(score[:, lo:hi], need[:, lo:hi], ACT.Tanh, scale=sens_t[:, i : i + 1])
            y = add_climate(i, lo, hi, score)
            if to_place is not None:
                place(*to_place)
            to_place = (i, lo, hi, y)
        place(*to_place)
